import numpy as np
import ml_dtypes


def mxq(x, axis, fmt="e4m3"):
    dtype, down = {"e4m3": (ml_dtypes.float8_e4m3fn, 7), "e5m2": (ml_dtypes.float8_e5m2, 14)}[fmt]
    v = np.moveaxis(np.asarray(x, np.float32).astype(ml_dtypes.bfloat16).astype(np.float64), axis, -1)
    blocks = v.reshape(v.shape[:-1] + (-1, 32))
    amax = np.abs(blocks).max(-1, keepdims=True)
    byte = np.maximum(np.where(amax > 0, np.frexp(amax)[1] - 1 + 127, 0) - down, 1)
    scale = np.exp2(byte - 127.0)
    codes = (blocks / scale).astype(np.float32).astype(dtype).astype(np.float64)
    return np.moveaxis((codes * scale).reshape(v.shape), -1, axis)


WIDE = False


def mx_kscale(k):
    if not WIDE:
        return np.ones(k)
    levels = np.array([30, -30])
    if k % 512:
        return np.exp2(np.random.permutation(np.resize(levels, k // 32))).repeat(32)
    a = np.empty((k // 512, 16))
    for p in range(k // 512):
        a[p, :8] = np.random.permutation(np.resize(levels, 8))
        for g in range(8):
            far = levels[np.abs(levels - a[p, g]) >= 10]
            a[p, g + 8] = far[np.random.randint(len(far))]
    return np.exp2(a.ravel()).repeat(32)


def f64(x):
    return np.asarray(x).astype(np.float64)


def striped(idx):
    return np.tile(np.asarray(idx).reshape(-1, 16).T, (8, 1)).astype(np.uint16)


def unstriped(offs):
    return offs[:16].T.reshape(-1).astype(np.int64)


def striped8(idx):
    return np.asarray(idx).reshape(8, -1, 16).transpose(0, 2, 1).reshape(128, -1).astype(np.uint16)


def unstriped8(offs):
    return offs.reshape(8, 16, -1).transpose(0, 2, 1).reshape(8, -1).astype(np.int64)


def pick8(x, idx, run):
    r = np.arange(len(x))
    return x[r[:, None], idx[r % (8 * run) // run]]


E2M1 = np.array([0.0, 0.5, 1.0, 1.5, 2.0, 3.0, 4.0, 6.0, -0.0, -0.5, -1.0, -1.5, -2.0, -3.0, -4.0, -6.0])


def pack_weight(w, fmt):
    k, n = w.shape
    w = f64(np.asarray(w, np.float32).astype(ml_dtypes.bfloat16)).reshape(k // 32, 32, n)
    amax = np.abs(w).max(1)
    if fmt in ("e4m3", "e5m2"):
        byte = np.frexp(amax)[1] - 1 + 127 - (7 if fmt == "e4m3" else 14)
    else:
        mant, ex = np.frexp(amax / 6.0)
        byte = np.where(mant > 0.5, ex, ex - 1) + 127
    byte = np.clip(np.where(amax > 0, byte, 1), 1, 254)
    scaled = (w * np.exp2(127.0 - byte)[:, None, :]).reshape(k, n).astype(np.float32)
    by_word = np.ascontiguousarray(scaled.reshape(k // 512, 128, 4, n).transpose(0, 1, 3, 2))
    if fmt in ("e4m3", "e5m2"):
        words = by_word.astype(ml_dtypes.float8_e4m3fn if fmt == "e4m3" else ml_dtypes.float8_e5m2).view(np.uint8)
    else:
        c = by_word.astype(ml_dtypes.float4_e2m1fn).view(np.uint8) & 0xF
        words = (c[..., 0::2] | (c[..., 1::2] << 4)).reshape(k // 512, 128, 2 * n)
    return np.ascontiguousarray(words), np.ascontiguousarray(byte.astype(np.uint8).reshape(k // 512, 16, n))


def unpack_weight(words, scales, fmt):
    g, _, n = scales.shape
    words = np.ascontiguousarray(words).reshape(g, 128, n, -1)
    if fmt in ("e4m3", "e5m2"):
        vals = words.view(ml_dtypes.float8_e4m3fn if fmt == "e4m3" else ml_dtypes.float8_e5m2).astype(np.float64)
    else:
        nib = np.empty((g, 128, n, 4), np.uint8)
        nib[..., 0::2] = words & 0xF
        nib[..., 1::2] = words >> 4
        vals = E2M1[nib]
    vals = vals * np.repeat(np.exp2(scales.astype(np.float64) - 127.0), 8, axis=1)[..., None]
    return vals.transpose(0, 1, 3, 2).reshape(g * 512, n)


K, T, J, R, F, Z, C, O, N, E = 512, 1024, 256, 512, 512, 1024, 512, 128, 256, 512


def setup_inputs():
    n = np.random.standard_normal
    idx = np.random.permutation(T)[:J]
    idx2 = np.random.permutation(Z)[:J]
    idx3 = np.stack([np.random.permutation(C)[:J] for _ in range(8)])
    idx4 = np.random.permutation(C)[:J]
    idx5 = np.random.permutation(J)[:O]
    idx6 = np.random.permutation(J)[:O]
    idx7 = np.stack([np.random.permutation(E)[:O] for _ in range(8)])
    fk = mx_kscale(K)
    ff = mx_kscale(F)
    fr = mx_kscale(R)
    xtp = pack_weight(n((K, T)) / fk[:, None], "e2m1")
    xop = pack_weight(n((F, Z)) / ff[:, None], "e5m2")
    wp = pack_weight(n((K, R)) * 1 / np.sqrt(K) * fk[:, None] * fr, "e5m2")
    w2p = pack_weight(n((K, R)) * 1 / np.sqrt(K) * fk[:, None] * fr, "e4m3")
    w0p = pack_weight(n((F, R)) * 1 / np.sqrt(F) * ff[:, None] * fr, "e4m3")
    wbp = pack_weight(n((R, N)) * 1 / np.sqrt(R) / fr[:, None], "e4m3")
    return {
        "xt_words": xtp[0],
        "xt_scales": xtp[1],
        "xo_words": xop[0],
        "xo_scales": xop[1],
        "w_words": wp[0],
        "w_scales": wp[1],
        "w2_words": w2p[0],
        "w2_scales": w2p[1],
        "w0_words": w0p[0],
        "w0_scales": w0p[1],
        "sa": (np.random.uniform(0.5, 1.6, (R, 1))).astype(np.float32),
        "sb": (np.random.uniform(0.5, 1.6, (R, 1))).astype(np.float32),
        "wb_words": wbp[0],
        "wb_scales": wbp[1],
        "offs": striped(idx),
        "offs2": striped(idx2),
        "offs3": striped8(idx3),
        "offs4": striped(idx4),
        "offs5": striped(idx5),
        "offs6": striped(idx6),
        "offs7": striped8(idx7),
    }


def reference(xt_words, xt_scales, xo_words, xo_scales, w_words, w_scales, w2_words, w2_scales, w0_words, w0_scales, sa, sb, wb_words, wb_scales, offs, offs2, offs3, offs4, offs5, offs6, offs7):
    idx = unstriped(offs)
    idx2 = unstriped(offs2)
    idx3 = unstriped8(offs3)
    idx4 = unstriped(offs4)
    idx5 = unstriped(offs5)
    idx6 = unstriped(offs6)
    idx7 = unstriped8(offs7)
    xtu = unpack_weight(xt_words, xt_scales, "e2m1")
    xou = unpack_weight(xo_words, xo_scales, "e5m2")
    wu = unpack_weight(w_words, w_scales, "e5m2")
    w2u = unpack_weight(w2_words, w2_scales, "e4m3")
    w0u = unpack_weight(w0_words, w0_scales, "e4m3")
    wbu = unpack_weight(wb_words, wb_scales, "e4m3")
    xtidxg = xtu[:, idx]
    a = wu.T @ xtidxg
    xoidx2g = xou[:, idx2]
    b = w2u.T @ xtidxg + w0u.T @ xoidx2g
    pw = np.zeros((R, C))
    pw[np.arange(R)[:, None], idx3[np.arange(R) % 512 // 64]] = a
    rb = np.maximum(pw[:, idx4] * f64(sa), b)
    hid = np.abs(rb[:, idx5] - rb[:, idx6] * f64(sb))
    hidq = mxq(hid, 0, "e5m2")
    p = wbu.T @ hidq
    y = np.zeros((N, E))
    y[np.arange(N)[:, None], idx7[np.arange(N) % 128 // 16]] = p
    return y

@@ -1,0 +1,190 @@
+from contextlib import ExitStack
+
+import concourse.mybir as mybir
+
+K, T, J, R, F, Z, C, O, N, E = 512, 1024, 256, 512, 512, 1024, 512, 128, 256, 512
+FLOPS = 2 * (K * R * J + K * R * J + F * R * J + R * N * O)
+
+F32 = mybir.dt.float32
+BF16 = mybir.dt.bfloat16
+I32 = mybir.dt.int32
+U32 = mybir.dt.uint32
+U16 = mybir.dt.uint16
+U8 = mybir.dt.uint8
+E4M3 = mybir.dt.float8_e4m3fn_x4
+E5M2 = mybir.dt.float8_e5m2_x4
+E2M1 = mybir.dt.float4_e2m1fn_x4
+ALU = mybir.AluOpType
+ACT = mybir.ActivationFunctionType
+
+P = 128
+PACK = 4
+QUADS = 4
+
+
+def tile_list_ownanswer_leaned_one_ownpage_kernel(
+    tc, xt_words, xt_scales, xo_words, xo_scales, w_words, w_scales, w2_words, w2_scales, w0_words, w0_scales,
+    sa, sb, wb_words, wb_scales, offs, offs2, offs3, offs4, offs5, offs6, offs7, out,
+):
+    nc = tc.nc
+    with ExitStack() as ctx:
+        keep = ctx.enter_context(tc.tile_pool(name="keep", bufs=1))
+        psum = ctx.enter_context(tc.psum_pool(name="psum", bufs=1))
+
+        def sbuf(shape, dtype, name):
+            return keep.tile(shape, dtype, name=name, align_bytes=64)
+
+        def load_list(src, name):
+            dst = keep.tile(list(src.shape), U16, name=name)
+            nc.sync.dma_start(dst[:], src)
+            return dst
+
+        def load_words(src, width, name):
+            dst = sbuf([P, width], U32, name)
+            nc.sync.dma_start(dst[:].bitcast(I32), src[0].rearrange("p n t -> p (n t)").bitcast(I32))
+            return dst
+
+        def zeroed_plane(width, name):
+            plane = sbuf([P, width], U8, name)
+            nc.vector.memset(plane[:].bitcast(I32), 0)
+            return plane
+
+        def stage_scales(src, width, name):
+            staged = sbuf([PACK, QUADS, width // 4], I32, name)
+            nc.sync.dma_start(staged[:], src[0].bitcast(I32).rearrange("(q r) c -> r q c", r=PACK))
+            return staged
+
+        def spread_scales(staged, plane):
+            for q in range(QUADS):
+                nc.vector.tensor_copy(plane[32 * q : 32 * q + PACK, :].bitcast(I32), staged[:, q, :])
+
+        def load_scales(src, plane):
+            rows = src[0].bitcast(I32).rearrange("(q r) c -> r q c", r=PACK)
+            for r in range(PACK):
+                nc.sync.dma_start(plane[r:P:32, :].bitcast(I32), rows[r])
+
+        def deal_bytes(plane, name):
+            dealt = sbuf([P, R], U8, name)
+            nc.vector.tensor_copy(
+                dealt[:].rearrange("p (t m) -> p t m", t=PACK), plane[:].rearrange("p (m t) -> p t m", t=PACK)
+            )
+            return dealt
+
+        def deal_words(copy, words, name):
+            dealt = sbuf([P, R], U32, name)
+            copy(dealt[:].rearrange("p (t m) -> p m t", t=PACK), words[:].rearrange("p (m t) -> p m t", t=PACK))
+            return dealt
+
+        xt_plane = zeroed_plane(T, "xt_plane")
+        w_plane = zeroed_plane(R, "w_plane")
+        xo_plane = zeroed_plane(Z, "xo_plane")
+        w2_plane = zeroed_plane(R, "w2_plane")
+        w0_plane = zeroed_plane(R, "w0_plane")
+        wb_plane = zeroed_plane(N, "wb_plane")
+
+        xt_staged = stage_scales(xt_scales, T, "xt_staged")
+        list1 = load_list(offs, "list1")
+        w_staged = stage_scales(w_scales, R, "w_staged")
+        xt_table = sbuf([P, T], U16, "xt_table")
+        nc.sync.dma_start(xt_table[:].bitcast(I32), xt_words[0].bitcast(I32))
+        w_raw = load_words(w_words, R, "w_raw")
+        list3 = load_list(offs3, "list3")
+        list2 = load_list(offs2, "list2")
+        xo_table = load_words(xo_words, Z, "xo_table")
+        load_scales(xo_scales, xo_plane)
+        w2_raw = load_words(w2_words, R, "w2_raw")
+        load_scales(w2_scales, w2_plane)
+        w0_raw = load_words(w0_words, R, "w0_raw")
+        load_scales(w0_scales, w0_plane)
+        list4 = load_list(offs4, "list4")
+        sa_cols = sbuf([P, PACK], F32, "sa_cols")
+        nc.sync.dma_start(sa_cols[:], sa.rearrange("(p t) one -> p (t one)", t=PACK))
+        list5 = load_list(offs5, "list5")
+        list6 = load_list(offs6, "list6")
+        sb_cols = sbuf([P, PACK], F32, "sb_cols")
+        nc.sync.dma_start(sb_cols[:], sb.rearrange("(p t) one -> p (t one)", t=PACK))
+        wb_codes = load_words(wb_words, N, "wb_codes")
+        load_scales(wb_scales, wb_plane)
+        list7 = load_list(offs7, "list7")
+
+        boards = [sbuf([P, C], F32, "board%d" % t) for t in range(PACK)]
+        pages = [sbuf([P, E], F32, "page%d" % h) for h in range(N // P)]
+        for cleared in boards + pages:
+            nc.vector.memset(cleared[:], 0.0)
+
+        spread_scales(w_staged, w_plane)
+        spread_scales(xt_staged, xt_plane)
+        w_bytes = deal_bytes(w_plane, "w_bytes")
+        xt_bytes = sbuf([P, J], U8, "xt_bytes")
+        nc.vector.tensor_copy(xt_bytes[:], xt_plane[:].indirect(list1[:]))
+        xt_codes = sbuf([P, J], U16, "xt_codes")
+        nc.vector.tensor_copy(xt_codes[:], xt_table[:].indirect(list1[:]))
+        w_codes = deal_words(nc.scalar.copy, w_raw, "w_codes")
+
+        firsts = []
+        for t in range(PACK):
+            cols = slice(t * P, (t + 1) * P)
+            a_sum = psum.tile([P, J], F32, name="a_sum", tag="a_sum", bufs=2)
+            nc.tensor.matmul_mx(
+                a_sum[:], lhsT=w_codes[:, cols].bitcast(E5M2), lhsT_scale=w_bytes[:, cols],
+                rhs=xt_codes[:].bitcast(E2M1), rhs_scale=xt_bytes[:], start=True, stop=True,
+            )
+            first = sbuf([P, J], F32, "first%d" % t)
+            nc.vector.tensor_copy(first[:], a_sum[:])
+            firsts.append(first)
+            nc.scalar.activation(boards[t][:].indirect(list3[:]), first[:], ACT.Copy)
+
+        xo_codes = sbuf([P, J], U32, "xo_codes")
+        nc.vector.tensor_copy(xo_codes[:], xo_table[:].indirect(list2[:]))
+        xo_bytes = sbuf([P, J], U8, "xo_bytes")
+        nc.vector.tensor_copy(xo_bytes[:], xo_plane[:].indirect(list2[:]))
+        w2_codes = deal_words(nc.vector.tensor_copy, w2_raw, "w2_codes")
+        w2_bytes = deal_bytes(w2_plane, "w2_bytes")
+        w0_codes = deal_words(nc.vector.tensor_copy, w0_raw, "w0_codes")
+        w0_bytes = deal_bytes(w0_plane, "w0_bytes")
+
+        answers = []
+        plain_picks = []
+        for t in range(PACK):
+            cols = slice(t * P, (t + 1) * P)
+            b_sum = psum.tile([P, J], F32, name="b_sum%d" % t)
+            nc.tensor.matmul_mx(
+                b_sum[:], lhsT=w2_codes[:, cols].bitcast(E4M3), lhsT_scale=w2_bytes[:, cols],
+                rhs=xt_codes[:].bitcast(E2M1), rhs_scale=xt_bytes[:], start=True, stop=False,
+            )
+            nc.tensor.matmul_mx(
+                b_sum[:], lhsT=w0_codes[:, cols].bitcast(E4M3), lhsT_scale=w0_bytes[:, cols],
+                rhs=xo_codes[:].bitcast(E5M2), rhs_scale=xo_bytes[:], start=False, stop=True,
+            )
+            leaned = sbuf([P, J], F32, "leaned%d" % t)
+            nc.scalar.activation(leaned[:], boards[t][:].indirect(list4[:]), ACT.Copy, scale=sa_cols[:, t : t + 1])
+            answer = sbuf([P, J], F32, "answer%d" % t)
+            nc.vector.tensor_tensor(answer[:], leaned[:], b_sum[:], ALU.max)
+            answers.append(answer)
+            plain = sbuf([P, O], F32, "plain%d" % t)
+            nc.vector.tensor_copy(plain[:], answer[:].indirect(list5[:]))
+            plain_picks.append(plain)
+
+        diff = sbuf([P, PACK, O], F32, "diff")
+        for t in range(PACK):
+            weighted = sbuf([P, O], F32, "weighted%d" % t)
+            nc.scalar.activation(weighted[:], answers[t][:].indirect(list6[:]), ACT.Copy, scale=sb_cols[:, t : t + 1])
+            nc.vector.tensor_tensor(diff[:, t, :], plain_picks[t][:], weighted[:], ALU.subtract)
+
+        hid = sbuf([P, O, PACK], BF16, "hid")
+        nc.scalar.activation(hid[:], diff[:].rearrange("p t o -> p o t"), ACT.Abs)
+        hid_codes = sbuf([P, O], U32, "hid_codes")
+        hid_bytes = sbuf([P, O], U8, "hid_bytes")
+        nc.vector.quantize_mx(hid_codes[:].bitcast(E5M2), hid_bytes[:], hid[:].rearrange("p o t -> p (o t)"))
+
+        for h in range(N // P):
+            cols = slice(h * P, (h + 1) * P)
+            p_sum = psum.tile([P, O], F32, name="p_sum%d" % h)
+            nc.tensor.matmul_mx(
+                p_sum[:], lhsT=wb_codes[:, cols].bitcast(E4M3), lhsT_scale=wb_plane[:, cols],
+                rhs=hid_codes[:].bitcast(E5M2), rhs_scale=hid_bytes[:], start=True, stop=True,
+            )
+            result = sbuf([P, O], F32, "result%d" % h)
+            nc.vector.tensor_copy(result[:], p_sum[:])
+            nc.scalar.activation(pages[h][:].indirect(list7[:]), result[:], ACT.Copy)
+            nc.sync.dma_start(out[cols, :], pages[h][:])

@@ -31,37 +31,37 @@ def tile_list_ownanswer_leaned_one_ownpage_kernel(
         keep = ctx.enter_context(tc.tile_pool(name="keep", bufs=1))
         psum = ctx.enter_context(tc.psum_pool(name="psum", bufs=1))
 
-        def sbuf(shape, dtype, name):
-            return keep.tile(shape, dtype, name=name, align_bytes=64)
+        def sbuf(shape, dtype, name, tag=""):
+            return keep.tile(shape, dtype, name=name, tag=tag or name, align_bytes=64)
 
         def load_list(src, name):
             dst = keep.tile(list(src.shape), U16, name=name)
             nc.sync.dma_start(dst[:], src)
             return dst
 
-        def load_words(src, width, name):
-            dst = sbuf([P, width], U32, name)
+        def load_words(src, width, name, tag=""):
+            dst = sbuf([P, width], U32, name, tag)
             nc.sync.dma_start(dst[:].bitcast(I32), src[0].rearrange("p n t -> p (n t)").bitcast(I32))
             return dst
 
-        def zeroed_plane(width, name):
-            plane = sbuf([P, width], U8, name)
+        def zeroed_plane(width, name, tag=""):
+            plane = sbuf([P, width], U8, name, tag)
             nc.vector.memset(plane[:].bitcast(I32), 0)
             return plane
 
-        def stage_scales(src, width, name):
+        def stage_scales(src, width, name, queue):
             staged = sbuf([PACK, QUADS, width // 4], I32, name)
-            nc.sync.dma_start(staged[:], src[0].bitcast(I32).rearrange("(q r) c -> r q c", r=PACK))
+            queue.dma_start(staged[:], src[0].bitcast(I32).rearrange("(q r) c -> r q c", r=PACK))
             return staged
 
         def spread_scales(staged, plane):
             for q in range(QUADS):
                 nc.vector.tensor_copy(plane[32 * q : 32 * q + PACK, :].bitcast(I32), staged[:, q, :])
 
-        def load_scales(src, plane):
+        def load_scales(src, plane, queue=nc.sync):
             rows = src[0].bitcast(I32).rearrange("(q r) c -> r q c", r=PACK)
             for r in range(PACK):
-                nc.sync.dma_start(plane[r:P:32, :].bitcast(I32), rows[r])
+                queue.dma_start(plane[r:P:32, :].bitcast(I32), rows[r])
 
         def deal_bytes(plane, name):
             dealt = sbuf([P, R], U8, name)
@@ -70,8 +70,8 @@ def tile_list_ownanswer_leaned_one_ownpage_kernel(
             )
             return dealt
 
-        def deal_words(copy, words, name):
-            dealt = sbuf([P, R], U32, name)
+        def deal_words(copy, words, name, tag):
+            dealt = sbuf([P, R], U32, name, tag)
             copy(dealt[:].rearrange("p (t m) -> p m t", t=PACK), words[:].rearrange("p (m t) -> p m t", t=PACK))
             return dealt
 
@@ -80,67 +80,95 @@ def tile_list_ownanswer_leaned_one_ownpage_kernel(
         xo_plane = zeroed_plane(Z, "xo_plane")
         w2_plane = zeroed_plane(R, "w2_plane")
         w0_plane = zeroed_plane(R, "w0_plane")
-        wb_plane = zeroed_plane(N, "wb_plane")
 
-        xt_staged = stage_scales(xt_scales, T, "xt_staged")
+        load_scales(xt_scales, xt_plane, nc.scalar)
+        w_staged = stage_scales(w_scales, R, "w_staged", nc.sync)
         list1 = load_list(offs, "list1")
-        w_staged = stage_scales(w_scales, R, "w_staged")
         xt_table = sbuf([P, T], U16, "xt_table")
         nc.sync.dma_start(xt_table[:].bitcast(I32), xt_words[0].bitcast(I32))
         w_raw = load_words(w_words, R, "w_raw")
         list3 = load_list(offs3, "list3")
-        list2 = load_list(offs2, "list2")
         xo_table = load_words(xo_words, Z, "xo_table")
-        load_scales(xo_scales, xo_plane)
         w2_raw = load_words(w2_words, R, "w2_raw")
-        load_scales(w2_scales, w2_plane)
         w0_raw = load_words(w0_words, R, "w0_raw")
-        load_scales(w0_scales, w0_plane)
         list4 = load_list(offs4, "list4")
         sa_cols = sbuf([P, PACK], F32, "sa_cols")
         nc.sync.dma_start(sa_cols[:], sa.rearrange("(p t) one -> p (t one)", t=PACK))
+        load_scales(xo_scales, xo_plane)
+        list2 = load_list(offs2, "list2")
+        load_scales(w2_scales, w2_plane)
+        load_scales(w0_scales, w0_plane)
         list5 = load_list(offs5, "list5")
         list6 = load_list(offs6, "list6")
-        sb_cols = sbuf([P, PACK], F32, "sb_cols")
-        nc.sync.dma_start(sb_cols[:], sb.rearrange("(p t) one -> p (t one)", t=PACK))
-        wb_codes = load_words(wb_words, N, "wb_codes")
-        load_scales(wb_scales, wb_plane)
         list7 = load_list(offs7, "list7")
 
-        boards = [sbuf([P, C], F32, "board%d" % t) for t in range(PACK)]
-        pages = [sbuf([P, E], F32, "page%d" % h) for h in range(N // P)]
-        for cleared in boards + pages:
-            nc.vector.memset(cleared[:], 0.0)
+        boards = [sbuf([P, C], F32, "board%d" % t) for t in range(2)]
+        for board in boards:
+            nc.gpsimd.memset(board[:], 0.0)
+
+        def deal_slot(copy, dealt, raw, slots):
+            copy(
+                dealt[:].rearrange("p (t m) -> p t m", t=PACK)[:, slots, :],
+                raw[:].rearrange("p (m t) -> p t m", t=PACK)[:, slots, :],
+            )
 
         spread_scales(w_staged, w_plane)
-        spread_scales(xt_staged, xt_plane)
-        w_bytes = deal_bytes(w_plane, "w_bytes")
         xt_bytes = sbuf([P, J], U8, "xt_bytes")
-        nc.vector.tensor_copy(xt_bytes[:], xt_plane[:].indirect(list1[:]))
         xt_codes = sbuf([P, J], U16, "xt_codes")
-        nc.vector.tensor_copy(xt_codes[:], xt_table[:].indirect(list1[:]))
-        w_codes = deal_words(nc.scalar.copy, w_raw, "w_codes")
+        w_bytes = sbuf([P, R], U8, "w_bytes")
+        w_codes = sbuf([P, R], U32, "w_codes")
+        halves = [slice(0, J // 2), slice(J // 2, J)]
+        entries = [slice(0, J // 32), slice(J // 32, J // 16)]
+        slot_sets = [slice(0, 1), slice(1, PACK)]
+        for u in range(2):
+            nc.vector.tensor_copy(xt_bytes[:, halves[u]], xt_plane[:].indirect(list1[:, entries[u]]))
+            deal_slot(nc.vector.tensor_copy, w_bytes, w_plane, slot_sets[u])
+            nc.vector.tensor_copy(xt_codes[:, halves[u]], xt_table[:].indirect(list1[:, entries[u]]))
+            deal_slot(nc.scalar.copy, w_codes, w_raw, slot_sets[u])
 
-        firsts = []
-        for t in range(PACK):
+        sb_cols = sbuf([P, PACK], F32, "sb_cols", "w_staged")
+        nc.sync.dma_start(sb_cols[:], sb.rearrange("(p t) one -> p (t one)", t=PACK))
+        wb_codes = load_words(wb_words, N, "wb_codes", "w_raw")
+        wb_plane = zeroed_plane(N, "wb_plane", "w_plane")
+        load_scales(wb_scales, wb_plane)
+
+        def place_first(t, js, copy):
             cols = slice(t * P, (t + 1) * P)
-            a_sum = psum.tile([P, J], F32, name="a_sum", tag="a_sum", bufs=2)
+            width = js.stop - js.start
+            a_sum = psum.tile([P, width], F32, name="a_sum", tag="a_sum", bufs=4)
             nc.tensor.matmul_mx(
                 a_sum[:], lhsT=w_codes[:, cols].bitcast(E5M2), lhsT_scale=w_bytes[:, cols],
-                rhs=xt_codes[:].bitcast(E2M1), rhs_scale=xt_bytes[:], start=True, stop=True,
+                rhs=xt_codes[:, js].bitcast(E2M1), rhs_scale=xt_bytes[:, js], start=True, stop=True,
             )
-            first = sbuf([P, J], F32, "first%d" % t)
-            nc.vector.tensor_copy(first[:], a_sum[:])
-            firsts.append(first)
-            nc.scalar.activation(boards[t][:].indirect(list3[:]), first[:], ACT.Copy)
+            first = sbuf([P, width], F32, "first%d_%d" % (t, js.start))
+            copy(first[:], a_sum[:])
+            nc.scalar.activation(boards[t % 2][:].indirect(list3[:, js.start // 16 : js.stop // 16]), first[:], ACT.Copy)
 
-        xo_codes = sbuf([P, J], U32, "xo_codes")
+        def fetch_leaned(t):
+            leaned = sbuf([P, J], F32, "leaned%d" % t)
+            nc.scalar.activation(leaned[:], boards[t % 2][:].indirect(list4[:]), ACT.Copy, scale=sa_cols[:, t : t + 1])
+            return leaned
+
+        place_first(0, halves[0], nc.scalar.copy)
+        place_first(1, halves[0], nc.vector.tensor_copy)
+        place_first(0, halves[1], nc.vector.tensor_copy)
+        place_first(1, halves[1], nc.vector.tensor_copy)
+        leans = [fetch_leaned(0), fetch_leaned(1)]
+        place_first(2, slice(0, J), nc.vector.tensor_copy)
+        place_first(3, slice(0, J), nc.vector.tensor_copy)
+        leans.extend([fetch_leaned(2), fetch_leaned(3)])
+
+        pages = [sbuf([P, E], F32, "page%d" % h, "board%d" % h) for h in range(N // P)]
+        for page in pages:
+            nc.gpsimd.memset(page[:], 0.0)
+
+        xo_codes = sbuf([P, J], U32, "xo_codes", "first0_128")
         nc.vector.tensor_copy(xo_codes[:], xo_table[:].indirect(list2[:]))
         xo_bytes = sbuf([P, J], U8, "xo_bytes")
         nc.vector.tensor_copy(xo_bytes[:], xo_plane[:].indirect(list2[:]))
-        w2_codes = deal_words(nc.vector.tensor_copy, w2_raw, "w2_codes")
+        w2_codes = deal_words(nc.vector.tensor_copy, w2_raw, "w2_codes", "first1_0")
         w2_bytes = deal_bytes(w2_plane, "w2_bytes")
-        w0_codes = deal_words(nc.vector.tensor_copy, w0_raw, "w0_codes")
+        w0_codes = deal_words(nc.vector.tensor_copy, w0_raw, "w0_codes", "first1_128")
         w0_bytes = deal_bytes(w0_plane, "w0_bytes")
 
         answers = []
@@ -156,20 +184,18 @@ def tile_list_ownanswer_leaned_one_ownpage_kernel(
                 b_sum[:], lhsT=w0_codes[:, cols].bitcast(E4M3), lhsT_scale=w0_bytes[:, cols],
                 rhs=xo_codes[:].bitcast(E5M2), rhs_scale=xo_bytes[:], start=False, stop=True,
             )
-            leaned = sbuf([P, J], F32, "leaned%d" % t)
-            nc.scalar.activation(leaned[:], boards[t][:].indirect(list4[:]), ACT.Copy, scale=sa_cols[:, t : t + 1])
             answer = sbuf([P, J], F32, "answer%d" % t)
-            nc.vector.tensor_tensor(answer[:], leaned[:], b_sum[:], ALU.max)
+            nc.vector.tensor_tensor(answer[:], leans[t][:], b_sum[:], ALU.max)
             answers.append(answer)
             plain = sbuf([P, O], F32, "plain%d" % t)
             nc.vector.tensor_copy(plain[:], answer[:].indirect(list5[:]))
             plain_picks.append(plain)
 
         diff = sbuf([P, PACK, O], F32, "diff")
+        weighted = sbuf([P, PACK, O], F32, "weighted", "leaned2")
         for t in range(PACK):
-            weighted = sbuf([P, O], F32, "weighted%d" % t)
-            nc.scalar.activation(weighted[:], answers[t][:].indirect(list6[:]), ACT.Copy, scale=sb_cols[:, t : t + 1])
-            nc.vector.tensor_tensor(diff[:, t, :], plain_picks[t][:], weighted[:], ALU.subtract)
+            nc.scalar.activation(weighted[:, t, :], answers[t][:].indirect(list6[:]), ACT.Copy, scale=sb_cols[:, t : t + 1])
+            nc.vector.tensor_tensor(diff[:, t, :], plain_picks[t][:], weighted[:, t, :], ALU.subtract)
 
         hid = sbuf([P, O, PACK], BF16, "hid")
         nc.scalar.activation(hid[:], diff[:].rearrange("p t o -> p o t"), ACT.Abs)
@@ -179,7 +205,7 @@ def tile_list_ownanswer_leaned_one_ownpage_kernel(
 
         for h in range(N // P):
             cols = slice(h * P, (h + 1) * P)
-            p_sum = psum.tile([P, O], F32, name="p_sum%d" % h)
+            p_sum = psum.tile([P, O], F32, name="p_sum", tag="a_sum", bufs=4)
             nc.tensor.matmul_mx(
                 p_sum[:], lhsT=wb_codes[:, cols].bitcast(E4M3), lhsT_scale=wb_plane[:, cols],
                 rhs=hid_codes[:].bitcast(E5M2), rhs_scale=hid_bytes[:], start=True, stop=True,

@@ -49,22 +49,22 @@ def tile_list_ownanswer_leaned_one_ownpage_kernel(
             nc.vector.memset(plane[:].bitcast(I32), 0)
             return plane
 
-        def stage_scales(src, width, name, queue):
+        def stage_scales(src, width, name):
             staged = sbuf([PACK, QUADS, width // 4], I32, name)
-            queue.dma_start(staged[:], src[0].bitcast(I32).rearrange("(q r) c -> r q c", r=PACK))
+            nc.sync.dma_start(staged[:], src[0].bitcast(I32).rearrange("(q r) c -> r q c", r=PACK))
             return staged
 
         def spread_scales(staged, plane):
             for q in range(QUADS):
                 nc.vector.tensor_copy(plane[32 * q : 32 * q + PACK, :].bitcast(I32), staged[:, q, :])
 
-        def load_scales(src, plane, queue=nc.sync):
+        def load_scales(src, plane, queues=(nc.sync,) * PACK):
             rows = src[0].bitcast(I32).rearrange("(q r) c -> r q c", r=PACK)
             for r in range(PACK):
-                queue.dma_start(plane[r:P:32, :].bitcast(I32), rows[r])
+                queues[r].dma_start(plane[r:P:32, :].bitcast(I32), rows[r])
 
-        def deal_bytes(plane, name):
-            dealt = sbuf([P, R], U8, name)
+        def deal_bytes(plane, name, tag):
+            dealt = sbuf([P, R], U8, name, tag)
             nc.vector.tensor_copy(
                 dealt[:].rearrange("p (t m) -> p t m", t=PACK), plane[:].rearrange("p (m t) -> p t m", t=PACK)
             )
@@ -77,39 +77,39 @@ def tile_list_ownanswer_leaned_one_ownpage_kernel(
 
         xt_plane = zeroed_plane(T, "xt_plane")
         w_plane = zeroed_plane(R, "w_plane")
-        xo_plane = zeroed_plane(Z, "xo_plane")
         w2_plane = zeroed_plane(R, "w2_plane")
+        xo_plane = zeroed_plane(Z, "xo_plane")
         w0_plane = zeroed_plane(R, "w0_plane")
 
-        load_scales(xt_scales, xt_plane, nc.scalar)
-        w_staged = stage_scales(w_scales, R, "w_staged", nc.sync)
+        w_staged = stage_scales(w_scales, R, "w_staged")
         list1 = load_list(offs, "list1")
+        load_scales(xt_scales, xt_plane, (nc.scalar, nc.scalar, nc.scalar, nc.sync))
         xt_table = sbuf([P, T], U16, "xt_table")
-        nc.sync.dma_start(xt_table[:].bitcast(I32), xt_words[0].bitcast(I32))
+        nc.scalar.dma_start(xt_table[:].bitcast(I32), xt_words[0].bitcast(I32))
         w_raw = load_words(w_words, R, "w_raw")
         list3 = load_list(offs3, "list3")
-        xo_table = load_words(xo_words, Z, "xo_table")
-        w2_raw = load_words(w2_words, R, "w2_raw")
-        w0_raw = load_words(w0_words, R, "w0_raw")
+        load_scales(w2_scales, w2_plane)
+        load_scales(xo_scales, xo_plane)
+        load_scales(w0_scales, w0_plane)
+        list2 = load_list(offs2, "list2")
         list4 = load_list(offs4, "list4")
         sa_cols = sbuf([P, PACK], F32, "sa_cols")
         nc.sync.dma_start(sa_cols[:], sa.rearrange("(p t) one -> p (t one)", t=PACK))
-        load_scales(xo_scales, xo_plane)
-        list2 = load_list(offs2, "list2")
-        load_scales(w2_scales, w2_plane)
-        load_scales(w0_scales, w0_plane)
+        w2_raw = load_words(w2_words, R, "w2_raw")
+        xo_table = load_words(xo_words, Z, "xo_table")
+        w0_raw = load_words(w0_words, R, "w0_raw")
         list5 = load_list(offs5, "list5")
         list6 = load_list(offs6, "list6")
         list7 = load_list(offs7, "list7")
 
         boards = [sbuf([P, C], F32, "board%d" % t) for t in range(2)]
         for board in boards:
-            nc.gpsimd.memset(board[:], 0.0)
+            nc.vector.memset(board[:], 0.0)
 
-        def deal_slot(copy, dealt, raw, slots):
+        def deal_slot(copy, dealt, raw, slots, order):
             copy(
-                dealt[:].rearrange("p (t m) -> p t m", t=PACK)[:, slots, :],
-                raw[:].rearrange("p (m t) -> p t m", t=PACK)[:, slots, :],
+                dealt.rearrange("p (t m) -> p t m", t=PACK)[:, slots, :].rearrange("p t m -> " + order),
+                raw.rearrange("p (m t) -> p t m", t=PACK)[:, slots, :].rearrange("p t m -> " + order),
             )
 
         spread_scales(w_staged, w_plane)
@@ -120,11 +120,14 @@ def tile_list_ownanswer_leaned_one_ownpage_kernel(
         halves = [slice(0, J // 2), slice(J // 2, J)]
         entries = [slice(0, J // 32), slice(J // 32, J // 16)]
         slot_sets = [slice(0, 1), slice(1, PACK)]
-        for u in range(2):
-            nc.vector.tensor_copy(xt_bytes[:, halves[u]], xt_plane[:].indirect(list1[:, entries[u]]))
-            deal_slot(nc.vector.tensor_copy, w_bytes, w_plane, slot_sets[u])
-            nc.vector.tensor_copy(xt_codes[:, halves[u]], xt_table[:].indirect(list1[:, entries[u]]))
-            deal_slot(nc.scalar.copy, w_codes, w_raw, slot_sets[u])
+        nc.vector.tensor_copy(xt_codes[:, halves[0]], xt_table[:].indirect(list1[:, entries[0]]))
+        deal_slot(nc.vector.tensor_copy, w_bytes[:], w_plane[:], slot_sets[0], "p t m")
+        nc.vector.tensor_copy(xt_bytes[:, halves[0]], xt_plane[:].indirect(list1[:, entries[0]]))
+        deal_slot(nc.vector.tensor_copy, w_bytes[:], w_plane[:], slot_sets[1], "p t m")
+        for slots in slot_sets:
+            deal_slot(nc.scalar.copy, w_codes[:], w_raw[:], slots, "p m t")
+        nc.vector.tensor_copy(xt_codes[:, halves[1]], xt_table[:].indirect(list1[:, entries[1]]))
+        nc.vector.tensor_copy(xt_bytes[:, halves[1]], xt_plane[:].indirect(list1[:, entries[1]]))
 
         sb_cols = sbuf([P, PACK], F32, "sb_cols", "w_staged")
         nc.sync.dma_start(sb_cols[:], sb.rearrange("(p t) one -> p (t one)", t=PACK))
@@ -158,34 +161,36 @@ def tile_list_ownanswer_leaned_one_ownpage_kernel(
         place_first(3, slice(0, J), nc.vector.tensor_copy)
         leans.extend([fetch_leaned(2), fetch_leaned(3)])
 
-        pages = [sbuf([P, E], F32, "page%d" % h, "board%d" % h) for h in range(N // P)]
+        pages = [sbuf([P, E], F32, "page%d" % h, "first%d_0" % (2 + h)) for h in range(N // P)]
         for page in pages:
             nc.gpsimd.memset(page[:], 0.0)
 
         xo_codes = sbuf([P, J], U32, "xo_codes", "first0_128")
         nc.vector.tensor_copy(xo_codes[:], xo_table[:].indirect(list2[:]))
-        xo_bytes = sbuf([P, J], U8, "xo_bytes")
+        xo_bytes = sbuf([P, J], U8, "xo_bytes", "xt_plane")
         nc.vector.tensor_copy(xo_bytes[:], xo_plane[:].indirect(list2[:]))
         w2_codes = deal_words(nc.vector.tensor_copy, w2_raw, "w2_codes", "first1_0")
-        w2_bytes = deal_bytes(w2_plane, "w2_bytes")
+        w2_bytes = deal_bytes(w2_plane, "w2_bytes", "first0_0")
         w0_codes = deal_words(nc.vector.tensor_copy, w0_raw, "w0_codes", "first1_128")
-        w0_bytes = deal_bytes(w0_plane, "w0_bytes")
+        w0_bytes = deal_bytes(w0_plane, "w0_bytes", "xt_table")
 
+        b_sums = [psum.tile([P, J], F32, name="b_sum%d" % t) for t in range(PACK)]
+        for t in range(PACK):
+            cols = slice(t * P, (t + 1) * P)
+            nc.tensor.matmul_mx(
+                b_sums[t][:], lhsT=w2_codes[:, cols].bitcast(E4M3), lhsT_scale=w2_bytes[:, cols],
+                rhs=xt_codes[:].bitcast(E2M1), rhs_scale=xt_bytes[:], start=True, stop=False,
+            )
         answers = []
         plain_picks = []
         for t in range(PACK):
             cols = slice(t * P, (t + 1) * P)
-            b_sum = psum.tile([P, J], F32, name="b_sum%d" % t)
             nc.tensor.matmul_mx(
-                b_sum[:], lhsT=w2_codes[:, cols].bitcast(E4M3), lhsT_scale=w2_bytes[:, cols],
-                rhs=xt_codes[:].bitcast(E2M1), rhs_scale=xt_bytes[:], start=True, stop=False,
-            )
-            nc.tensor.matmul_mx(
-                b_sum[:], lhsT=w0_codes[:, cols].bitcast(E4M3), lhsT_scale=w0_bytes[:, cols],
+                b_sums[t][:], lhsT=w0_codes[:, cols].bitcast(E4M3), lhsT_scale=w0_bytes[:, cols],
                 rhs=xo_codes[:].bitcast(E5M2), rhs_scale=xo_bytes[:], start=False, stop=True,
             )
             answer = sbuf([P, J], F32, "answer%d" % t)
-            nc.vector.tensor_tensor(answer[:], leans[t][:], b_sum[:], ALU.max)
+            nc.vector.tensor_tensor(answer[:], leans[t][:], b_sums[t][:], ALU.max)
             answers.append(answer)
             plain = sbuf([P, O], F32, "plain%d" % t)
             nc.vector.tensor_copy(plain[:], answer[:].indirect(list5[:]))

@@ -51,7 +51,7 @@ def tile_list_ownanswer_leaned_one_ownpage_kernel(
 
         def stage_scales(src, width, name):
             staged = sbuf([PACK, QUADS, width // 4], I32, name)
-            nc.sync.dma_start(staged[:], src[0].bitcast(I32).rearrange("(q r) c -> r q c", r=PACK))
+            nc.scalar.dma_start(staged[:], src[0].bitcast(I32).rearrange("(q r) c -> r q c", r=PACK))
             return staged
 
         def spread_scales(staged, plane):
@@ -83,18 +83,18 @@ def tile_list_ownanswer_leaned_one_ownpage_kernel(
 
         w_staged = stage_scales(w_scales, R, "w_staged")
         list1 = load_list(offs, "list1")
-        load_scales(xt_scales, xt_plane, (nc.scalar, nc.scalar, nc.scalar, nc.sync))
         xt_table = sbuf([P, T], U16, "xt_table")
-        nc.scalar.dma_start(xt_table[:].bitcast(I32), xt_words[0].bitcast(I32))
+        nc.sync.dma_start(xt_table[:].bitcast(I32), xt_words[0].bitcast(I32))
+        load_scales(xt_scales, xt_plane, (nc.scalar, nc.scalar, nc.scalar, nc.sync))
         w_raw = load_words(w_words, R, "w_raw")
         list3 = load_list(offs3, "list3")
+        list4 = load_list(offs4, "list4")
+        sa_cols = sbuf([P, PACK], F32, "sa_cols")
+        nc.sync.dma_start(sa_cols[:], sa.rearrange("(p t) one -> p (t one)", t=PACK))
         load_scales(w2_scales, w2_plane)
         load_scales(xo_scales, xo_plane)
         load_scales(w0_scales, w0_plane)
         list2 = load_list(offs2, "list2")
-        list4 = load_list(offs4, "list4")
-        sa_cols = sbuf([P, PACK], F32, "sa_cols")
-        nc.sync.dma_start(sa_cols[:], sa.rearrange("(p t) one -> p (t one)", t=PACK))
         w2_raw = load_words(w2_words, R, "w2_raw")
         xo_table = load_words(xo_words, Z, "xo_table")
         w0_raw = load_words(w0_words, R, "w0_raw")
@@ -167,12 +167,12 @@ def tile_list_ownanswer_leaned_one_ownpage_kernel(
 
         xo_codes = sbuf([P, J], U32, "xo_codes", "first0_128")
         nc.vector.tensor_copy(xo_codes[:], xo_table[:].indirect(list2[:]))
-        xo_bytes = sbuf([P, J], U8, "xo_bytes", "xt_plane")
+        xo_bytes = sbuf([P, J], U8, "xo_bytes", "w_codes")
         nc.vector.tensor_copy(xo_bytes[:], xo_plane[:].indirect(list2[:]))
         w2_codes = deal_words(nc.vector.tensor_copy, w2_raw, "w2_codes", "first1_0")
         w2_bytes = deal_bytes(w2_plane, "w2_bytes", "first0_0")
         w0_codes = deal_words(nc.vector.tensor_copy, w0_raw, "w0_codes", "first1_128")
-        w0_bytes = deal_bytes(w0_plane, "w0_bytes", "xt_table")
+        w0_bytes = deal_bytes(w0_plane, "w0_bytes", "w_bytes")
 
         b_sums = [psum.tile([P, J], F32, name="b_sum%d" % t) for t in range(PACK)]
         for t in range(PACK):
@@ -203,7 +203,9 @@ def tile_list_ownanswer_leaned_one_ownpage_kernel(
             nc.vector.tensor_tensor(diff[:, t, :], plain_picks[t][:], weighted[:, t, :], ALU.subtract)
 
         hid = sbuf([P, O, PACK], BF16, "hid")
-        nc.scalar.activation(hid[:], diff[:].rearrange("p t o -> p o t"), ACT.Abs)
+        by_place = diff[:].rearrange("p t o -> p o t")
+        nc.scalar.activation(hid[:, :, 2:4], by_place[:, :, 2:4], ACT.Abs)
+        nc.vector.scalar_tensor_tensor(hid[:, :, 0:2], by_place[:, :, 0:2], -1.0, by_place[:, :, 0:2], ALU.mult, ALU.max)
         hid_codes = sbuf([P, O], U32, "hid_codes")
         hid_bytes = sbuf([P, O], U8, "hid_bytes")
         nc.vector.quantize_mx(hid_codes[:].bitcast(E5M2), hid_bytes[:], hid[:].rearrange("p o t -> p (o t)"))

from contextlib import ExitStack

import concourse.mybir as mybir

K, T, J, R, F, Z, C, O, N, E = 512, 1024, 256, 512, 512, 1024, 512, 128, 256, 512
FLOPS = 2 * (K * R * J + K * R * J + F * R * J + R * N * O)

F32 = mybir.dt.float32
BF16 = mybir.dt.bfloat16
I32 = mybir.dt.int32
U32 = mybir.dt.uint32
U16 = mybir.dt.uint16
U8 = mybir.dt.uint8
E4M3 = mybir.dt.float8_e4m3fn_x4
E5M2 = mybir.dt.float8_e5m2_x4
E2M1 = mybir.dt.float4_e2m1fn_x4
ALU = mybir.AluOpType
ACT = mybir.ActivationFunctionType

P = 128
PACK = 4
QUADS = 4


def tile_list_ownanswer_leaned_one_ownpage_kernel(
    tc, xt_words, xt_scales, xo_words, xo_scales, w_words, w_scales, w2_words, w2_scales, w0_words, w0_scales,
    sa, sb, wb_words, wb_scales, offs, offs2, offs3, offs4, offs5, offs6, offs7, out,
):
    nc = tc.nc
    with ExitStack() as ctx:
        keep = ctx.enter_context(tc.tile_pool(name="keep", bufs=1))
        psum = ctx.enter_context(tc.psum_pool(name="psum", bufs=1))

        def sbuf(shape, dtype, name, tag=""):
            return keep.tile(shape, dtype, name=name, tag=tag or name, align_bytes=64)

        def load_list(src, name):
            dst = keep.tile(list(src.shape), U16, name=name)
            nc.sync.dma_start(dst[:], src)
            return dst

        def load_words(src, width, name, tag=""):
            dst = sbuf([P, width], U32, name, tag)
            nc.sync.dma_start(dst[:].bitcast(I32), src[0].rearrange("p n t -> p (n t)").bitcast(I32))
            return dst

        def zeroed_plane(width, name, tag=""):
            plane = sbuf([P, width], U8, name, tag)
            nc.vector.memset(plane[:].bitcast(I32), 0)
            return plane

        def stage_scales(src, width, name):
            staged = sbuf([PACK, QUADS, width // 4], I32, name)
            nc.scalar.dma_start(staged[:], src[0].bitcast(I32).rearrange("(q r) c -> r q c", r=PACK))
            return staged

        def spread_scales(staged, plane):
            for q in range(QUADS):
                nc.vector.tensor_copy(plane[32 * q : 32 * q + PACK, :].bitcast(I32), staged[:, q, :])

        def load_scales(src, plane, queues=(nc.sync,) * PACK):
            rows = src[0].bitcast(I32).rearrange("(q r) c -> r q c", r=PACK)
            for r in range(PACK):
                queues[r].dma_start(plane[r:P:32, :].bitcast(I32), rows[r])

        def deal_bytes(plane, name, tag):
            dealt = sbuf([P, R], U8, name, tag)
            nc.vector.tensor_copy(
                dealt[:].rearrange("p (t m) -> p t m", t=PACK), plane[:].rearrange("p (m t) -> p t m", t=PACK)
            )
            return dealt

        def deal_words(copy, words, name, tag):
            dealt = sbuf([P, R], U32, name, tag)
            copy(dealt[:].rearrange("p (t m) -> p m t", t=PACK), words[:].rearrange("p (m t) -> p m t", t=PACK))
            return dealt

        xt_plane = zeroed_plane(T, "xt_plane")
        w_plane = zeroed_plane(R, "w_plane")
        w2_plane = zeroed_plane(R, "w2_plane")
        xo_plane = zeroed_plane(Z, "xo_plane")
        w0_plane = zeroed_plane(R, "w0_plane")

        w_staged = stage_scales(w_scales, R, "w_staged")
        list1 = load_list(offs, "list1")
        xt_table = sbuf([P, T], U16, "xt_table")
        nc.sync.dma_start(xt_table[:].bitcast(I32), xt_words[0].bitcast(I32))
        load_scales(xt_scales, xt_plane, (nc.scalar, nc.scalar, nc.scalar, nc.sync))
        w_raw = load_words(w_words, R, "w_raw")
        list3 = load_list(offs3, "list3")
        list4 = load_list(offs4, "list4")
        sa_cols = sbuf([P, PACK], F32, "sa_cols")
        nc.sync.dma_start(sa_cols[:], sa.rearrange("(p t) one -> p (t one)", t=PACK))
        load_scales(w2_scales, w2_plane)
        load_scales(xo_scales, xo_plane)
        load_scales(w0_scales, w0_plane)
        list2 = load_list(offs2, "list2")
        w2_raw = load_words(w2_words, R, "w2_raw")
        xo_table = load_words(xo_words, Z, "xo_table")
        w0_raw = load_words(w0_words, R, "w0_raw")
        list5 = load_list(offs5, "list5")
        list6 = load_list(offs6, "list6")
        list7 = load_list(offs7, "list7")

        boards = [sbuf([P, C], F32, "board%d" % t) for t in range(2)]
        for board in boards:
            nc.vector.memset(board[:], 0.0)

        def deal_slot(copy, dealt, raw, slots, order):
            copy(
                dealt.rearrange("p (t m) -> p t m", t=PACK)[:, slots, :].rearrange("p t m -> " + order),
                raw.rearrange("p (m t) -> p t m", t=PACK)[:, slots, :].rearrange("p t m -> " + order),
            )

        spread_scales(w_staged, w_plane)
        xt_bytes = sbuf([P, J], U8, "xt_bytes")
        xt_codes = sbuf([P, J], U16, "xt_codes")
        w_bytes = sbuf([P, R], U8, "w_bytes")
        w_codes = sbuf([P, R], U32, "w_codes")
        halves = [slice(0, J // 2), slice(J // 2, J)]
        entries = [slice(0, J // 32), slice(J // 32, J // 16)]
        slot_sets = [slice(0, 1), slice(1, PACK)]
        nc.vector.tensor_copy(xt_codes[:, halves[0]], xt_table[:].indirect(list1[:, entries[0]]))
        deal_slot(nc.vector.tensor_copy, w_bytes[:], w_plane[:], slot_sets[0], "p t m")
        nc.vector.tensor_copy(xt_bytes[:, halves[0]], xt_plane[:].indirect(list1[:, entries[0]]))
        deal_slot(nc.vector.tensor_copy, w_bytes[:], w_plane[:], slot_sets[1], "p t m")
        for slots in slot_sets:
            deal_slot(nc.scalar.copy, w_codes[:], w_raw[:], slots, "p m t")
        nc.vector.tensor_copy(xt_codes[:, halves[1]], xt_table[:].indirect(list1[:, entries[1]]))
        nc.vector.tensor_copy(xt_bytes[:, halves[1]], xt_plane[:].indirect(list1[:, entries[1]]))

        sb_cols = sbuf([P, PACK], F32, "sb_cols", "w_staged")
        nc.sync.dma_start(sb_cols[:], sb.rearrange("(p t) one -> p (t one)", t=PACK))
        wb_codes = load_words(wb_words, N, "wb_codes", "w_raw")
        wb_plane = zeroed_plane(N, "wb_plane", "w_plane")
        load_scales(wb_scales, wb_plane)

        def place_first(t, js, copy):
            cols = slice(t * P, (t + 1) * P)
            width = js.stop - js.start
            a_sum = psum.tile([P, width], F32, name="a_sum", tag="a_sum", bufs=4)
            nc.tensor.matmul_mx(
                a_sum[:], lhsT=w_codes[:, cols].bitcast(E5M2), lhsT_scale=w_bytes[:, cols],
                rhs=xt_codes[:, js].bitcast(E2M1), rhs_scale=xt_bytes[:, js], start=True, stop=True,
            )
            first = sbuf([P, width], F32, "first%d_%d" % (t, js.start))
            copy(first[:], a_sum[:])
            nc.scalar.activation(boards[t % 2][:].indirect(list3[:, js.start // 16 : js.stop // 16]), first[:], ACT.Copy)

        def fetch_leaned(t):
            leaned = sbuf([P, J], F32, "leaned%d" % t)
            nc.scalar.activation(leaned[:], boards[t % 2][:].indirect(list4[:]), ACT.Copy, scale=sa_cols[:, t : t + 1])
            return leaned

        place_first(0, halves[0], nc.scalar.copy)
        place_first(1, halves[0], nc.vector.tensor_copy)
        place_first(0, halves[1], nc.vector.tensor_copy)
        place_first(1, halves[1], nc.vector.tensor_copy)
        leans = [fetch_leaned(0), fetch_leaned(1)]
        place_first(2, slice(0, J), nc.vector.tensor_copy)
        place_first(3, slice(0, J), nc.vector.tensor_copy)
        leans.extend([fetch_leaned(2), fetch_leaned(3)])

        pages = [sbuf([P, E], F32, "page%d" % h, "first%d_0" % (2 + h)) for h in range(N // P)]
        for page in pages:
            nc.gpsimd.memset(page[:], 0.0)

        xo_codes = sbuf([P, J], U32, "xo_codes", "first0_128")
        nc.vector.tensor_copy(xo_codes[:], xo_table[:].indirect(list2[:]))
        xo_bytes = sbuf([P, J], U8, "xo_bytes", "w_codes")
        nc.vector.tensor_copy(xo_bytes[:], xo_plane[:].indirect(list2[:]))
        w2_codes = deal_words(nc.vector.tensor_copy, w2_raw, "w2_codes", "first1_0")
        w2_bytes = deal_bytes(w2_plane, "w2_bytes", "first0_0")
        w0_codes = deal_words(nc.vector.tensor_copy, w0_raw, "w0_codes", "first1_128")
        w0_bytes = deal_bytes(w0_plane, "w0_bytes", "w_bytes")

        b_sums = [psum.tile([P, J], F32, name="b_sum%d" % t) for t in range(PACK)]
        for t in range(PACK):
            cols = slice(t * P, (t + 1) * P)
            nc.tensor.matmul_mx(
                b_sums[t][:], lhsT=w2_codes[:, cols].bitcast(E4M3), lhsT_scale=w2_bytes[:, cols],
                rhs=xt_codes[:].bitcast(E2M1), rhs_scale=xt_bytes[:], start=True, stop=False,
            )
        answers = []
        plain_picks = []
        for t in range(PACK):
            cols = slice(t * P, (t + 1) * P)
            nc.tensor.matmul_mx(
                b_sums[t][:], lhsT=w0_codes[:, cols].bitcast(E4M3), lhsT_scale=w0_bytes[:, cols],
                rhs=xo_codes[:].bitcast(E5M2), rhs_scale=xo_bytes[:], start=False, stop=True,
            )
            answer = sbuf([P, J], F32, "answer%d" % t)
            nc.vector.tensor_tensor(answer[:], leans[t][:], b_sums[t][:], ALU.max)
            answers.append(answer)
            plain = sbuf([P, O], F32, "plain%d" % t)
            nc.vector.tensor_copy(plain[:], answer[:].indirect(list5[:]))
            plain_picks.append(plain)

        diff = sbuf([P, PACK, O], F32, "diff")
        weighted = sbuf([P, PACK, O], F32, "weighted", "leaned2")
        for t in range(PACK):
            nc.scalar.activation(weighted[:, t, :], answers[t][:].indirect(list6[:]), ACT.Copy, scale=sb_cols[:, t : t + 1])
            nc.vector.tensor_tensor(diff[:, t, :], plain_picks[t][:], weighted[:, t, :], ALU.subtract)

        hid = sbuf([P, O, PACK], BF16, "hid")
        by_place = diff[:].rearrange("p t o -> p o t")
        nc.scalar.activation(hid[:, :, 2:4], by_place[:, :, 2:4], ACT.Abs)
        nc.vector.scalar_tensor_tensor(hid[:, :, 0:2], by_place[:, :, 0:2], -1.0, by_place[:, :, 0:2], ALU.mult, ALU.max)
        hid_codes = sbuf([P, O], U32, "hid_codes")
        hid_bytes = sbuf([P, O], U8, "hid_bytes")
        nc.vector.quantize_mx(hid_codes[:].bitcast(E5M2), hid_bytes[:], hid[:].rearrange("p o t -> p (o t)"))

        for h in range(N // P):
            cols = slice(h * P, (h + 1) * P)
            p_sum = psum.tile([P, O], F32, name="p_sum", tag="a_sum", bufs=4)
            nc.tensor.matmul_mx(
                p_sum[:], lhsT=wb_codes[:, cols].bitcast(E4M3), lhsT_scale=wb_plane[:, cols],
                rhs=hid_codes[:].bitcast(E5M2), rhs_scale=hid_bytes[:], start=True, stop=True,
            )
            result = sbuf([P, O], F32, "result%d" % h)
            nc.vector.tensor_copy(result[:], p_sum[:])
            nc.scalar.activation(pages[h][:].indirect(list7[:]), result[:], ACT.Copy)
            nc.sync.dma_start(out[cols, :], pages[h][:])
